import numpy as np
import ml_dtypes


def mxq(x, axis, fmt="e4m3"):
    dtype, down = {"e4m3": (ml_dtypes.float8_e4m3fn, 7), "e5m2": (ml_dtypes.float8_e5m2, 14)}[fmt]
    v = np.moveaxis(np.asarray(x, np.float32).astype(ml_dtypes.bfloat16).astype(np.float64), axis, -1)
    blocks = v.reshape(v.shape[:-1] + (-1, 32))
    amax = np.abs(blocks).max(-1, keepdims=True)
    byte = np.maximum(np.where(amax > 0, np.frexp(amax)[1] - 1 + 127, 0) - down, 1)
    scale = np.exp2(byte - 127.0)
    codes = (blocks / scale).astype(np.float32).astype(dtype).astype(np.float64)
    return np.moveaxis((codes * scale).reshape(v.shape), -1, axis)


WIDE = False


def mx_kscale(k):
    if not WIDE:
        return np.ones(k)
    levels = np.array([10, -10, 5, -5, 0])
    if k % 512:
        return np.exp2(np.random.permutation(np.resize(levels, k // 32))).repeat(32)
    a = np.empty((k // 512, 16))
    for p in range(k // 512):
        a[p, :8] = np.random.permutation(np.resize(levels, 8))
        for g in range(8):
            far = levels[np.abs(levels - a[p, g]) >= 10]
            a[p, g + 8] = far[np.random.randint(len(far))]
    return np.exp2(a.ravel()).repeat(32)


def f64(x):
    return np.asarray(x).astype(np.float64)


def striped(idx):
    return np.tile(idx.reshape(-1, 16).T, (8, 1)).astype(np.uint16)


def unstriped(offs):
    return offs[:16].T.reshape(-1).astype(np.int64)


def pack_weight(w):
    k, n = w.shape
    w = f64(np.asarray(w, np.float32).astype(ml_dtypes.bfloat16)).reshape(k // 32, 32, n)
    amax = np.abs(w).max(1)
    byte = np.clip(np.where(amax > 0, np.frexp(amax)[1] - 1 + 127 - 7, 1), 1, 254)
    scaled = (w * np.exp2(127.0 - byte)[:, None, :]).reshape(k, n).astype(np.float32)
    words = np.ascontiguousarray(scaled.reshape(k // 512, 128, 4, n).transpose(0, 1, 3, 2)).astype(ml_dtypes.float8_e4m3fn).view(np.uint8)
    return words, np.ascontiguousarray(byte.astype(np.uint8).reshape(k // 512, 16, n))


def unpack_weight(words, scales):
    g, p, n, _ = words.shape
    vals = np.ascontiguousarray(words).view(ml_dtypes.float8_e4m3fn).astype(np.float64) * np.repeat(np.exp2(scales.astype(np.float64) - 127.0), 8, axis=1)[..., None]
    return vals.transpose(0, 1, 3, 2).reshape(g * 512, n)


K, T, S, N, H = 1024, 2048, 512, 256, 512


def setup_inputs():
    n = np.random.standard_normal
    s = mx_kscale(K)[:, None]
    u = mx_kscale(H)
    packed_xT = pack_weight(n((K, T)) * s)
    return {
        "x_words": packed_xT[0],
        "x_scales": packed_xT[1],
        "w1": (n((K, H)) / np.sqrt(K) / s).astype(np.float32),
        "w2": (n((K, H)) / np.sqrt(K) / s).astype(np.float32),
        "kpin": (np.random.uniform(0.2, 0.6, (H, 1))).astype(np.float32),
        "unit": (np.random.uniform(0.6, 1.4, (H, 1)) * u[:, None]).astype(np.float32),
        "w3": (n((H, N)) / np.sqrt(H) / u[:, None]).astype(np.float32),
        "offs": striped(np.random.permutation(T)[:S]),
        "nn1": striped(np.random.permutation(S)),
        "nn2": striped(np.random.permutation(S)),
    }


def reference(x_words, x_scales, w1, w2, kpin, unit, w3, offs, nn1, nn2):
    xq = unpack_weight(x_words, x_scales)[:, unstriped(offs)]
    mg = mxq(f64(w2), 0, "e4m3").T @ xq
    mag = np.tanh(mg)
    hf = mxq(f64(w1), 0, "e4m3").T @ xq
    m1 = mag[:, unstriped(nn1)]
    m2 = mag[:, unstriped(nn2)]
    heff = hf + 0.6 * mag + 0.3 * (m1 + m2)
    anh = heff / (np.abs(heff) + 0.8)
    pin = (anh - mag) / (np.abs(anh - mag) + 0.4)
    irr = mag + f64(kpin) * pin
    hid = f64(unit) * (irr + 0.4 * anh)
    return mxq(f64(w3), 0, "e4m3").T @ mxq(hid, 0, "e4m3")

@@ -1,0 +1,272 @@
+from contextlib import ExitStack
+
+import concourse.mybir as mybir
+
+K, T, S, N, H = 1024, 2048, 512, 256, 512
+FLOPS = 2 * (2 * K * H * S + H * N * S)
+
+F32 = mybir.dt.float32
+BF16 = mybir.dt.bfloat16
+I32 = mybir.dt.int32
+U32 = mybir.dt.uint32
+U16 = mybir.dt.uint16
+U8 = mybir.dt.uint8
+FP8X4 = mybir.dt.float8_e4m3fn_x4
+ACT = mybir.ActivationFunctionType
+ALU = mybir.AluOpType
+
+P = 128
+PACK = 4
+K_PASS = P * PACK
+PASSES = K // K_PASS
+GROUPS = [(0, 256, [(0, 2), (2, 2)]), (256, 384, [(0, 4)]), (384, 512, [(0, 2), (2, 2)])]
+W_ON_V = (0,)
+E_ON_S = ()
+IL_ON_S = (0,)
+REUSE = {"one2": "w1_1_bf16", "one3": "anh1", "one4": "both2", "a11": "a10"}
+ABS_ON_V = (0,)
+
+
+def tile_picked_yhystr_sum_p_kernel(
+    tc, x_words, x_scales, w1, w2, kpin, unit, w3, offs, nn1, nn2, out
+):
+    nc = tc.nc
+    with ExitStack() as ctx:
+        keep = ctx.enter_context(tc.tile_pool(name="keep", bufs=1))
+        psum = ctx.enter_context(tc.psum_pool(name="psum", bufs=1))
+
+        def sb(name, shape, dtype):
+            return keep.tile(shape, dtype, name=name, tag=REUSE.get(name, name), align_bytes=64)
+
+        def clock(name, ap):
+            probe = sb("probe_" + name, [P, 1], F32)
+            nc.gpsimd.tensor_copy(out=probe[:], in_=ap)
+
+        offs_sb = keep.tile([P, S // 16], U16, name="offs_sb")
+        nn1_sb = keep.tile([P, S // 16], U16, name="nn1_sb")
+        nn2_sb = keep.tile([P, S // 16], U16, name="nn2_sb")
+
+        x_planes = sb("x_planes", [P, T], U8)
+        nc.gpsimd.memset(x_planes[:].bitcast(I32), 0)
+        for q in range(4):
+            nc.scalar.dma_start(
+                out=x_planes[32 * q : 32 * q + 8, :].bitcast(I32),
+                in_=x_scales[:, 4 * q : 4 * q + 4, :].bitcast(I32),
+            )
+        kpin_sb = sb("kpin_sb", [P, PACK], F32)
+        unit_sb = sb("unit_sb", [P, PACK], F32)
+
+        def load_rows(name, rows):
+            raw = sb(name, [P, PACK, rows.shape[1]], F32)
+            nc.sync.dma_start(out=raw[:], in_=rows.rearrange("(p j) c -> p j c", j=PACK))
+            return raw
+
+        def load_words(o):
+            words = sb("x_table%d" % o, [P, T], I32)
+            nc.sync.dma_start(out=words[:], in_=x_words[o].rearrange("p n t -> p (n t)").bitcast(I32))
+            return words
+
+        w2_raw = [load_rows("w2_raw0", w2[0:K_PASS, :])]
+        nc.sync.dma_start(offs_sb[:], offs)
+        x_table = [load_words(0)]
+        w2_raw.append(load_rows("w2_raw1", w2[K_PASS:K, :]))
+        x_table.append(load_words(1))
+        w1_raw = [load_rows("w1_raw0", w1[0:K_PASS, :])]
+        nc.sync.dma_start(nn1_sb[:], nn1)
+        nc.sync.dma_start(nn2_sb[:], nn2)
+        w1_raw.append(load_rows("w1_raw1", w1[K_PASS:K, :]))
+        w3_raw = load_rows("w3_raw", w3)
+        nc.sync.dma_start(out=kpin_sb[:], in_=kpin.rearrange("(p t) o -> p (t o)", t=PACK))
+        nc.sync.dma_start(out=unit_sb[:], in_=unit.rearrange("(p t) o -> p (t o)", t=PACK))
+
+        def quantise(name, grouped, width):
+            codes = sb(name + "_codes", [P, width], U32)
+            scales = sb(name + "_scales", [P, width], U8)
+            nc.vector.quantize_mx(out=codes[:].bitcast(FP8X4), scales=scales[:], in_=grouped)
+            return codes, scales
+
+        def move(on_scalar, dst, src):
+            if on_scalar:
+                nc.scalar.activation(out=dst, in_=src, func=ACT.Copy)
+            else:
+                nc.vector.tensor_copy(out=dst, in_=src)
+
+        def round_dealt(name, raw, on_scalar):
+            grouped = sb(name + "_bf16", [P, PACK * H], BF16)
+            dst = grouped[:].rearrange("p (t m j) -> p m j t", t=PACK, j=PACK)
+            src = raw[:].rearrange("p j (m t) -> p m j t", t=PACK)
+            move(on_scalar, dst, src)
+            return grouped
+
+        def gather_words(o):
+            picked = sb("x_picked%d" % o, [P, S], U32)
+            nc.vector.tensor_copy(out=picked[:], in_=x_table[o][:].bitcast(U32).indirect(offs_sb[:]))
+            return picked
+
+        w2_q = [quantise("w2_0", round_dealt("w2_0", w2_raw[0], False)[:], H)]
+        x_scale = sb("x_scale", [P, S], U8)
+        nc.vector.tensor_copy(out=x_scale[:], in_=x_planes[:].indirect(offs_sb[:]))
+        x_picked = [gather_words(0)]
+        w2_q.append(quantise("w2_1", round_dealt("w2_1", w2_raw[1], False)[:], H))
+        x_picked.append(gather_words(1))
+
+        def product(acc, w_q, o, t, cols):
+            codes, scales = w_q[o]
+            nc.tensor.matmul_mx(
+                out=acc,
+                lhsT=codes[:, t * P : (t + 1) * P].bitcast(FP8X4),
+                lhsT_scale=scales[:, t * P : (t + 1) * P],
+                rhs=x_picked[o][:, cols].bitcast(FP8X4),
+                rhs_scale=x_scale[4 * o : P, cols],
+                start=(o == 0),
+                stop=(o == PASSES - 1),
+            )
+
+        mg = [psum.tile([P, S], F32, name="mg%d" % t, tag="bank%d" % t) for t in range(PACK)]
+        for o in range(PASSES):
+            for t in range(PACK):
+                product(mg[t][:], w2_q, o, t, slice(0, S))
+
+        mag = sb("mag", [P, PACK, S], F32)
+        half_mag = [sb("half_mag%d" % t, [P, S], F32) for t in range(PACK)]
+        for t in range(PACK):
+            nc.scalar.activation(out=mag[:, t, :], in_=mg[t][:], func=ACT.Tanh)
+            if t in W_ON_V:
+                nc.vector.tensor_scalar(out=half_mag[t][:], in0=mag[:, t, :], scalar1=0.5, scalar2=None, op0=ALU.mult)
+            else:
+                nc.scalar.activation(out=half_mag[t][:], in_=mag[:, t, :], func=ACT.Copy, scale=0.5)
+
+
+        w1_q = [quantise("w1_0", round_dealt("w1_0", w1_raw[0], False)[:], H)]
+        w1_q.append(quantise("w1_1", round_dealt("w1_1", w1_raw[1], True)[:], H))
+
+        units = []
+        for g, (c0, c1, parts) in enumerate(GROUPS):
+            for t0, nt in parts:
+                units.append((g, c0, c1, t0, nt))
+
+        hf = []
+        filled = 512
+        bank = 3
+        for n, (g, c0, c1, t0, nt) in enumerate(units):
+            width = nt * (c1 - c0)
+            if filled + width > 512:
+                bank = bank + 1
+                acc = psum.tile([P, 512], F32, name="hf%d" % bank, tag="bank%d" % bank)
+                filled = 0
+            view = acc[:, filled : filled + width].rearrange("p (t c) -> p t c", t=nt)
+            filled = filled + width
+            for i in range(nt):
+                for o in range(PASSES):
+                    product(view[:, i, :], w1_q, o, t0 + i, slice(c0, c1))
+            hf.append(view)
+
+        pin_gain = sb("pin_gain", [P, PACK], F32)
+        slip_gain = sb("slip_gain", [P, PACK], F32)
+        mag_gain = sb("mag_gain", [P, PACK], F32)
+        w3_bf16 = sb("w3_bf16", [P, PACK * N], BF16)
+        w3_q = []
+
+        def late_constants():
+            nc.vector.scalar_tensor_tensor(
+                out=pin_gain[:], in0=kpin_sb[:], scalar=2.5, in1=unit_sb[:], op0=ALU.mult, op1=ALU.mult
+            )
+            nc.vector.tensor_scalar(out=slip_gain[:], in0=unit_sb[:], scalar1=0.4, scalar2=None, op0=ALU.mult)
+            nc.vector.tensor_scalar(out=mag_gain[:], in0=unit_sb[:], scalar1=1.4, scalar2=None, op0=ALU.mult)
+            nc.scalar.activation(
+                out=w3_bf16[:].rearrange("p (c i j) -> p c j i", i=4, j=PACK),
+                in_=w3_raw[:].rearrange("p j (c i) -> p c j i", i=4),
+                func=ACT.Copy,
+            )
+
+        hid = [sb("hid%d" % g, [P, PACK, c1 - c0], F32) for g, (c0, c1, parts) in enumerate(GROUPS)]
+
+        def chain(n):
+            g, c0, c1, t0, nt = units[n]
+
+            def wt(name):
+                return sb("%s%d" % (name, n), [P, nt, c1 - c0], F32)
+
+            mag_n = mag[:, t0 : t0 + nt, c0:c1]
+            one, both, u = wt("one"), wt("both"), wt("u")
+            entries = slice(c0 // 16, c1 // 16)
+            for i in range(nt):
+                nc.vector.tensor_tensor(
+                    one[:, i, :], half_mag[t0 + i][:].indirect(nn1_sb[:, entries]), mag_n[:, i, :], ALU.add
+                )
+            for i in range(nt):
+                nc.vector.tensor_tensor(
+                    both[:, i, :], half_mag[t0 + i][:].indirect(nn2_sb[:, entries]), one[:, i, :], ALU.add
+                )
+            nc.vector.scalar_tensor_tensor(
+                out=u[:], in0=hf[n], scalar=1.0 / 0.6, in1=both[:], op0=ALU.mult, op1=ALU.add
+            )
+
+            a, q, r = wt("a1"), wt("q1"), wt("r1")
+            if n in ABS_ON_V:
+                nc.vector.scalar_tensor_tensor(out=a[:], in0=u[:], scalar=-1.0, in1=u[:], op0=ALU.mult, op1=ALU.max)
+            else:
+                nc.scalar.activation(out=a[:], in_=u[:], func=ACT.Abs)
+            nc.scalar.activation(out=q[:], in_=a[:], func=ACT.Abs_reciprocal_sqrt, scale=0.75, bias=1.0)
+            nc.scalar.activation(out=r[:], in_=q[:], func=ACT.Square)
+            anh, d = wt("anh"), wt("d")
+            nc.vector.scalar_tensor_tensor(out=anh[:], in0=u[:], scalar=0.75, in1=r[:], op0=ALU.mult, op1=ALU.mult)
+            nc.vector.tensor_tensor(d[:], anh[:], mag_n, ALU.subtract)
+            if n == 0:
+                late_constants()
+            a2, q2, r2, e = wt("a2"), wt("q2"), wt("r2"), wt("e")
+            nc.scalar.activation(out=a2[:], in_=d[:], func=ACT.Abs)
+            nc.scalar.activation(out=q2[:], in_=a2[:], func=ACT.Square, scale=2.5, bias=1.0)
+            nc.scalar.activation(out=r2[:], in_=q2[:], func=ACT.Abs_reciprocal_sqrt)
+            for i in range(nt):
+                t = t0 + i
+                if n in E_ON_S:
+                    nc.scalar.activation(
+                        out=e[:, i, :], in_=r2[:, i, :], func=ACT.Identity,
+                        scale=pin_gain[:, t : t + 1], bias=slip_gain[:, t : t + 1],
+                    )
+                else:
+                    nc.vector.tensor_scalar(
+                        out=e[:, i, :], in0=r2[:, i, :], scalar1=pin_gain[:, t : t + 1],
+                        scalar2=slip_gain[:, t : t + 1], op0=ALU.mult, op1=ALU.add,
+                    )
+            f = wt("f")
+            nc.vector.tensor_tensor(f[:], d[:], e[:], ALU.mult)
+            for i in range(nt):
+                t = t0 + i
+                nc.vector.scalar_tensor_tensor(
+                    out=hid[g][:, t, :], in0=mag_n[:, i, :], scalar=mag_gain[:, t : t + 1],
+                    in1=f[:, i, :], op0=ALU.mult, op1=ALU.add,
+                )
+
+        def coils(g):
+            c0, c1, parts = GROUPS[g]
+            width = c1 - c0
+            if g == 0:
+                w3_q.extend(quantise("w3", w3_bf16[:], N))
+            grouped = sb("hid_bf16_%d" % g, [P, PACK * width], BF16)
+            move(
+                g in IL_ON_S,
+                grouped[:].rearrange("p (c i t) -> p c t i", i=4, t=PACK),
+                hid[g][:].rearrange("p t (c i) -> p c t i", i=4),
+            )
+            codes, scales = quantise("hid%d" % g, grouped[:], width)
+            acc = psum.tile([P, 2, width], F32, name="coil%d" % g, tag="bank%d" % g)
+            for m in range(2):
+                nc.tensor.matmul_mx(
+                    out=acc[:, m, :],
+                    lhsT=w3_q[0][:, m * P : (m + 1) * P].bitcast(FP8X4),
+                    lhsT_scale=w3_q[1][:, m * P : (m + 1) * P],
+                    rhs=codes[:].bitcast(FP8X4),
+                    rhs_scale=scales[:],
+                    start=True,
+                    stop=True,
+                )
+            result = sb("result%d" % g, [P, 2, width], F32)
+            nc.scalar.activation(out=result[:], in_=acc[:], func=ACT.Copy)
+            nc.sync.dma_start(out=out[:, c0:c1].rearrange("(m p) c -> p m c", p=P), in_=result[:])
+
+        for n, (g, c0, c1, t0, nt) in enumerate(units):
+            chain(n)
+            if t0 + nt == PACK:
+                coils(g)

@@ -19,12 +19,15 @@ P = 128
 PACK = 4
 K_PASS = P * PACK
 PASSES = K // K_PASS
-GROUPS = [(0, 256, [(0, 2), (2, 2)]), (256, 384, [(0, 4)]), (384, 512, [(0, 2), (2, 2)])]
-W_ON_V = (0,)
-E_ON_S = ()
-IL_ON_S = (0,)
-REUSE = {"one2": "w1_1_bf16", "one3": "anh1", "one4": "both2", "a11": "a10"}
+UNITS = [(0, 0, 512), (1, 0, 512), (2, 0, 512), (3, 0, 256), (3, 256, 384), (3, 384, 512)]
+GROUPS = [(0, 256), (256, 384), (384, 512)]
+GATHER_ON_S = (2, 3)
+GAIN = "XVXVSV"
+IL = "SVS"
+EV = "SSV"
 ABS_ON_V = (0,)
+REUSE = {"a1_1": "a1_0"}
+PAD = 16
 
 
 def tile_picked_yhystr_sum_p_kernel(
@@ -47,12 +50,7 @@ def tile_picked_yhystr_sum_p_kernel(
         nn2_sb = keep.tile([P, S // 16], U16, name="nn2_sb")
 
         x_planes = sb("x_planes", [P, T], U8)
-        nc.gpsimd.memset(x_planes[:].bitcast(I32), 0)
-        for q in range(4):
-            nc.scalar.dma_start(
-                out=x_planes[32 * q : 32 * q + 8, :].bitcast(I32),
-                in_=x_scales[:, 4 * q : 4 * q + 4, :].bitcast(I32),
-            )
+        nc.vector.memset(x_planes[:].bitcast(I32), 0)
         kpin_sb = sb("kpin_sb", [P, PACK], F32)
         unit_sb = sb("unit_sb", [P, PACK], F32)
 
@@ -67,6 +65,11 @@ def tile_picked_yhystr_sum_p_kernel(
             return words
 
         w2_raw = [load_rows("w2_raw0", w2[0:K_PASS, :])]
+        for q in range(4):
+            nc.sync.dma_start(
+                out=x_planes[32 * q : 32 * q + 8, :].bitcast(I32),
+                in_=x_scales[:, 4 * q : 4 * q + 4, :].bitcast(I32),
+            )
         nc.sync.dma_start(offs_sb[:], offs)
         x_table = [load_words(0)]
         w2_raw.append(load_rows("w2_raw1", w2[K_PASS:K, :]))
@@ -104,9 +107,9 @@ def tile_picked_yhystr_sum_p_kernel(
             return picked
 
         w2_q = [quantise("w2_0", round_dealt("w2_0", w2_raw[0], False)[:], H)]
+        x_picked = [gather_words(0)]
         x_scale = sb("x_scale", [P, S], U8)
         nc.vector.tensor_copy(out=x_scale[:], in_=x_planes[:].indirect(offs_sb[:]))
-        x_picked = [gather_words(0)]
         w2_q.append(quantise("w2_1", round_dealt("w2_1", w2_raw[1], False)[:], H))
         x_picked.append(gather_words(1))
 
@@ -127,39 +130,29 @@ def tile_picked_yhystr_sum_p_kernel(
             for t in range(PACK):
                 product(mg[t][:], w2_q, o, t, slice(0, S))
 
-        mag = sb("mag", [P, PACK, S], F32)
-        half_mag = [sb("half_mag%d" % t, [P, S], F32) for t in range(PACK)]
+        mag = []
+        window = []
         for t in range(PACK):
-            nc.scalar.activation(out=mag[:, t, :], in_=mg[t][:], func=ACT.Tanh)
-            if t in W_ON_V:
-                nc.vector.tensor_scalar(out=half_mag[t][:], in0=mag[:, t, :], scalar1=0.5, scalar2=None, op0=ALU.mult)
+            table = sb("window%d" % t, [P, S + PAD], F32)
+            nc.vector.memset(table[:, S:], 0.0)
+            window.append(table)
+            if t in GATHER_ON_S:
+                mag.append(table[:, :S])
+                nc.scalar.activation(out=mag[t], in_=mg[t][:], func=ACT.Tanh)
             else:
-                nc.scalar.activation(out=half_mag[t][:], in_=mag[:, t, :], func=ACT.Copy, scale=0.5)
+                plain = sb("mag%d" % t, [P, S], F32)
+                mag.append(plain[:])
+                nc.scalar.activation(out=mag[t], in_=mg[t][:], func=ACT.Tanh)
+                nc.scalar.activation(out=table[:, :S], in_=mag[t], func=ACT.Copy, scale=0.5)
 
 
         w1_q = [quantise("w1_0", round_dealt("w1_0", w1_raw[0], False)[:], H)]
-        w1_q.append(quantise("w1_1", round_dealt("w1_1", w1_raw[1], True)[:], H))
+        w1_q.append(quantise("w1_1", round_dealt("w1_1", w1_raw[1], False)[:], H))
 
-        units = []
-        for g, (c0, c1, parts) in enumerate(GROUPS):
-            for t0, nt in parts:
-                units.append((g, c0, c1, t0, nt))
-
-        hf = []
-        filled = 512
-        bank = 3
-        for n, (g, c0, c1, t0, nt) in enumerate(units):
-            width = nt * (c1 - c0)
-            if filled + width > 512:
-                bank = bank + 1
-                acc = psum.tile([P, 512], F32, name="hf%d" % bank, tag="bank%d" % bank)
-                filled = 0
-            view = acc[:, filled : filled + width].rearrange("p (t c) -> p t c", t=nt)
-            filled = filled + width
-            for i in range(nt):
-                for o in range(PASSES):
-                    product(view[:, i, :], w1_q, o, t0 + i, slice(c0, c1))
-            hf.append(view)
+        hf = [psum.tile([P, S], F32, name="hf%d" % t, tag="bank%d" % (PACK + t)) for t in range(PACK)]
+        for t in range(PACK):
+            for o in range(PASSES):
+                product(hf[t][:], w1_q, o, t, slice(0, S))
 
         pin_gain = sb("pin_gain", [P, PACK], F32)
         slip_gain = sb("slip_gain", [P, PACK], F32)
@@ -179,27 +172,38 @@ def tile_picked_yhystr_sum_p_kernel(
                 func=ACT.Copy,
             )
 
-        hid = [sb("hid%d" % g, [P, PACK, c1 - c0], F32) for g, (c0, c1, parts) in enumerate(GROUPS)]
+        hid = sb("hid", [P, PACK, S], F32)
+        near = {}
+
+        def neighbours(t):
+            one = sb("one%d" % t, [P, S], F32)
+            both = sb("both%d" % t, [P, S], F32)
+            if t in GATHER_ON_S:
+                two = sb("two%d" % t, [P, S], F32)
+                pair = sb("pair%d" % t, [P, S], F32)
+                nc.scalar.activation(one[:], window[t][:].indirect(nn1_sb[:]), ACT.Copy)
+                nc.scalar.activation(two[:], window[t][:].indirect(nn2_sb[:]), ACT.Copy)
+                nc.vector.tensor_tensor(pair[:], one[:], two[:], ALU.add)
+                nc.vector.scalar_tensor_tensor(
+                    out=both[:], in0=pair[:], scalar=0.5, in1=mag[t], op0=ALU.mult, op1=ALU.add
+                )
+            else:
+                nc.vector.tensor_tensor(one[:], window[t][:].indirect(nn1_sb[:]), mag[t], ALU.add)
+                nc.vector.tensor_tensor(both[:], window[t][:].indirect(nn2_sb[:]), one[:], ALU.add)
+            near[t] = both
 
         def chain(n):
-            g, c0, c1, t0, nt = units[n]
+            t, c0, c1 = UNITS[n]
 
             def wt(name):
-                return sb("%s%d" % (name, n), [P, nt, c1 - c0], F32)
+                return sb("%s_%d" % (name, n), [P, c1 - c0], F32)
 
-            mag_n = mag[:, t0 : t0 + nt, c0:c1]
-            one, both, u = wt("one"), wt("both"), wt("u")
-            entries = slice(c0 // 16, c1 // 16)
-            for i in range(nt):
-                nc.vector.tensor_tensor(
-                    one[:, i, :], half_mag[t0 + i][:].indirect(nn1_sb[:, entries]), mag_n[:, i, :], ALU.add
-                )
-            for i in range(nt):
-                nc.vector.tensor_tensor(
-                    both[:, i, :], half_mag[t0 + i][:].indirect(nn2_sb[:, entries]), one[:, i, :], ALU.add
-                )
+            if t not in near:
+                neighbours(t)
+            mag_n = mag[t][:, c0:c1]
+            u = wt("u")
             nc.vector.scalar_tensor_tensor(
-                out=u[:], in0=hf[n], scalar=1.0 / 0.6, in1=both[:], op0=ALU.mult, op1=ALU.add
+                out=u[:], in0=hf[t][:, c0:c1], scalar=1.0 / 0.6, in1=near[t][:, c0:c1], op0=ALU.mult, op1=ALU.add
             )
 
             a, q, r = wt("a1"), wt("q1"), wt("r1")
@@ -214,41 +218,46 @@ def tile_picked_yhystr_sum_p_kernel(
             nc.vector.tensor_tensor(d[:], anh[:], mag_n, ALU.subtract)
             if n == 0:
                 late_constants()
-            a2, q2, r2, e = wt("a2"), wt("q2"), wt("r2"), wt("e")
+            a2, q2, e, f = wt("a2"), wt("q2"), wt("e"), wt("f")
             nc.scalar.activation(out=a2[:], in_=d[:], func=ACT.Abs)
-            nc.scalar.activation(out=q2[:], in_=a2[:], func=ACT.Square, scale=2.5, bias=1.0)
-            nc.scalar.activation(out=r2[:], in_=q2[:], func=ACT.Abs_reciprocal_sqrt)
-            for i in range(nt):
-                t = t0 + i
-                if n in E_ON_S:
+            if GAIN[n] == "X":
+                nc.scalar.activation(out=q2[:], in_=a2[:], func=ACT.Abs_reciprocal_sqrt, scale=2.5, bias=1.0)
+                nc.vector.scalar_tensor_tensor(
+                    out=e[:], in0=q2[:], scalar=pin_gain[:, t : t + 1], in1=q2[:], op0=ALU.mult, op1=ALU.mult
+                )
+                nc.vector.scalar_tensor_tensor(
+                    out=f[:], in0=e[:], scalar=slip_gain[:, t : t + 1], in1=d[:], op0=ALU.add, op1=ALU.mult
+                )
+            else:
+                r2 = wt("r2")
+                nc.scalar.activation(out=q2[:], in_=a2[:], func=ACT.Square, scale=2.5, bias=1.0)
+                nc.scalar.activation(out=r2[:], in_=q2[:], func=ACT.Abs_reciprocal_sqrt)
+                if GAIN[n] == "S":
                     nc.scalar.activation(
-                        out=e[:, i, :], in_=r2[:, i, :], func=ACT.Identity,
+                        out=e[:], in_=r2[:], func=ACT.Identity,
                         scale=pin_gain[:, t : t + 1], bias=slip_gain[:, t : t + 1],
                     )
                 else:
                     nc.vector.tensor_scalar(
-                        out=e[:, i, :], in0=r2[:, i, :], scalar1=pin_gain[:, t : t + 1],
+                        out=e[:], in0=r2[:], scalar1=pin_gain[:, t : t + 1],
                         scalar2=slip_gain[:, t : t + 1], op0=ALU.mult, op1=ALU.add,
                     )
-            f = wt("f")
-            nc.vector.tensor_tensor(f[:], d[:], e[:], ALU.mult)
-            for i in range(nt):
-                t = t0 + i
-                nc.vector.scalar_tensor_tensor(
-                    out=hid[g][:, t, :], in0=mag_n[:, i, :], scalar=mag_gain[:, t : t + 1],
-                    in1=f[:, i, :], op0=ALU.mult, op1=ALU.add,
-                )
+                nc.vector.tensor_tensor(f[:], d[:], e[:], ALU.mult)
+            nc.vector.scalar_tensor_tensor(
+                out=hid[:, t, c0:c1], in0=mag_n, scalar=mag_gain[:, t : t + 1], in1=f[:], op0=ALU.mult, op1=ALU.add
+            )
+
 
         def coils(g):
-            c0, c1, parts = GROUPS[g]
+            c0, c1 = GROUPS[g]
             width = c1 - c0
             if g == 0:
                 w3_q.extend(quantise("w3", w3_bf16[:], N))
             grouped = sb("hid_bf16_%d" % g, [P, PACK * width], BF16)
             move(
-                g in IL_ON_S,
+                IL[g] == "S",
                 grouped[:].rearrange("p (c i t) -> p c t i", i=4, t=PACK),
-                hid[g][:].rearrange("p t (c i) -> p c t i", i=4),
+                hid[:, :, c0:c1].rearrange("p t (c i) -> p c t i", i=4),
             )
             codes, scales = quantise("hid%d" % g, grouped[:], width)
             acc = psum.tile([P, 2, width], F32, name="coil%d" % g, tag="bank%d" % g)
@@ -263,10 +272,12 @@ def tile_picked_yhystr_sum_p_kernel(
                     stop=True,
                 )
             result = sb("result%d" % g, [P, 2, width], F32)
-            nc.scalar.activation(out=result[:], in_=acc[:], func=ACT.Copy)
+            move(EV[g] == "S", result[:], acc[:])
             nc.sync.dma_start(out=out[:, c0:c1].rearrange("(m p) c -> p m c", p=P), in_=result[:])
 
-        for n, (g, c0, c1, t0, nt) in enumerate(units):
+        for n, (t, c0, c1) in enumerate(UNITS):
             chain(n)
-            if t0 + nt == PACK:
-                coils(g)
+            if t == PACK - 1:
+                for g, (g0, g1) in enumerate(GROUPS):
+                    if c0 < g1 <= c1:
+                        coils(g)

@@ -17,17 +17,19 @@ ALU = mybir.AluOpType
 
 P = 128
 PACK = 4
+RUN = 4
 K_PASS = P * PACK
 PASSES = K // K_PASS
-UNITS = [(0, 0, 512), (1, 0, 512), (2, 0, 512), (3, 0, 256), (3, 256, 384), (3, 384, 512)]
-GROUPS = [(0, 256), (256, 384), (384, 512)]
-GATHER_ON_S = (2, 3)
-GAIN = "XVXVSV"
-IL = "SVS"
-EV = "SSV"
-ABS_ON_V = (0,)
-REUSE = {"a1_1": "a1_0"}
-PAD = 16
+QUADRANT = 32
+SPARE = 16
+FACTOR_PITCH = 8
+OUT_COLS = 128
+
+FIRST_TILE_ON_SCALAR = 2
+
+CHAINS = [(t, 0, S) for t in range(PACK - 1)] + [(PACK - 1, 0, S // 2), (PACK - 1, S // 2, S)]
+
+REUSE = {"abs_u_1": "abs_u_0", "pin_gain": "root_u_0", "slip_gain": "inv_u_0", "mag_gain": "anh_0"}
 
 
 def tile_picked_yhystr_sum_p_kernel(
@@ -41,86 +43,84 @@ def tile_picked_yhystr_sum_p_kernel(
         def sb(name, shape, dtype):
             return keep.tile(shape, dtype, name=name, tag=REUSE.get(name, name), align_bytes=64)
 
-        def clock(name, ap):
-            probe = sb("probe_" + name, [P, 1], F32)
-            nc.gpsimd.tensor_copy(out=probe[:], in_=ap)
-
         offs_sb = keep.tile([P, S // 16], U16, name="offs_sb")
         nn1_sb = keep.tile([P, S // 16], U16, name="nn1_sb")
         nn2_sb = keep.tile([P, S // 16], U16, name="nn2_sb")
 
-        x_planes = sb("x_planes", [P, T], U8)
-        nc.vector.memset(x_planes[:].bitcast(I32), 0)
-        kpin_sb = sb("kpin_sb", [P, PACK], F32)
-        unit_sb = sb("unit_sb", [P, PACK], F32)
+        scale_table = sb("scale_table", [P, T], U8)
+        nc.vector.memset(scale_table[:].bitcast(I32), 0)
+        kpin_sb = sb("kpin_sb", [P, PACK, FACTOR_PITCH], F32)
+        unit_sb = sb("unit_sb", [P, PACK, FACTOR_PITCH], F32)
 
-        def load_rows(name, rows):
-            raw = sb(name, [P, PACK, rows.shape[1]], F32)
+        def load_pass(name, w, o):
+            raw = sb("%s_raw%d" % (name, o), [P, PACK, H], F32)
+            rows = w[o * K_PASS : (o + 1) * K_PASS, :]
             nc.sync.dma_start(out=raw[:], in_=rows.rearrange("(p j) c -> p j c", j=PACK))
             return raw
 
         def load_words(o):
-            words = sb("x_table%d" % o, [P, T], I32)
-            nc.sync.dma_start(out=words[:], in_=x_words[o].rearrange("p n t -> p (n t)").bitcast(I32))
+            words = sb("word_table%d" % o, [P, T], I32)
+            nc.sync.dma_start(out=words[:], in_=x_words[o].rearrange("p n j -> p (n j)").bitcast(I32))
             return words
 
-        w2_raw = [load_rows("w2_raw0", w2[0:K_PASS, :])]
-        for q in range(4):
+        def by_tile(rows):
+            return rows.rearrange("(g t e) n -> t g e n", t=PACK, e=RUN)
+
+        w2_raw = [load_pass("w2", w2, 0)]
+        for q in range(P // QUADRANT):
             nc.sync.dma_start(
-                out=x_planes[32 * q : 32 * q + 8, :].bitcast(I32),
+                out=scale_table[QUADRANT * q : QUADRANT * q + 4 * PASSES, :].bitcast(I32),
                 in_=x_scales[:, 4 * q : 4 * q + 4, :].bitcast(I32),
             )
         nc.sync.dma_start(offs_sb[:], offs)
-        x_table = [load_words(0)]
-        w2_raw.append(load_rows("w2_raw1", w2[K_PASS:K, :]))
-        x_table.append(load_words(1))
-        w1_raw = [load_rows("w1_raw0", w1[0:K_PASS, :])]
+        word_table = [load_words(0)]
+        w2_raw.append(load_pass("w2", w2, 1))
+        word_table.append(load_words(1))
+        w1_raw = [load_pass("w1", w1, 0)]
         nc.sync.dma_start(nn1_sb[:], nn1)
         nc.sync.dma_start(nn2_sb[:], nn2)
-        w1_raw.append(load_rows("w1_raw1", w1[K_PASS:K, :]))
-        w3_raw = load_rows("w3_raw", w3)
-        nc.sync.dma_start(out=kpin_sb[:], in_=kpin.rearrange("(p t) o -> p (t o)", t=PACK))
-        nc.sync.dma_start(out=unit_sb[:], in_=unit.rearrange("(p t) o -> p (t o)", t=PACK))
+        w1_raw.append(load_pass("w1", w1, 1))
+        w3_raw = sb("w3_raw", [P, PACK, N], F32)
+        for t in range(PACK):
+            nc.sync.dma_start(out=w3_raw[:, t, :], in_=by_tile(w3)[t])
+        for t in range(PACK):
+            nc.sync.dma_start(out=kpin_sb[:, t, 0:1], in_=by_tile(kpin)[t])
+            nc.sync.dma_start(out=unit_sb[:, t, 0:1], in_=by_tile(unit)[t])
 
-        def quantise(name, grouped, width):
+        def quantise(name, rounded, width):
             codes = sb(name + "_codes", [P, width], U32)
             scales = sb(name + "_scales", [P, width], U8)
-            nc.vector.quantize_mx(out=codes[:].bitcast(FP8X4), scales=scales[:], in_=grouped)
+            nc.vector.quantize_mx(out=codes[:].bitcast(FP8X4), scales=scales[:], in_=rounded[:])
             return codes, scales
 
-        def move(on_scalar, dst, src):
-            if on_scalar:
-                nc.scalar.activation(out=dst, in_=src, func=ACT.Copy)
-            else:
-                nc.vector.tensor_copy(out=dst, in_=src)
-
-        def round_dealt(name, raw, on_scalar):
-            grouped = sb(name + "_bf16", [P, PACK * H], BF16)
-            dst = grouped[:].rearrange("p (t m j) -> p m j t", t=PACK, j=PACK)
-            src = raw[:].rearrange("p j (m t) -> p m j t", t=PACK)
-            move(on_scalar, dst, src)
-            return grouped
+        def quantise_pass(name, raw):
+            rounded = sb(name + "_bf16", [P, PACK * H], BF16)
+            nc.vector.tensor_copy(
+                out=rounded[:].rearrange("p (t g e j) -> p g t j e", t=PACK, e=RUN, j=PACK),
+                in_=raw[:].rearrange("p j (g t e) -> p g t j e", t=PACK, e=RUN),
+            )
+            return quantise(name, rounded, H)
 
         def gather_words(o):
             picked = sb("x_picked%d" % o, [P, S], U32)
-            nc.vector.tensor_copy(out=picked[:], in_=x_table[o][:].bitcast(U32).indirect(offs_sb[:]))
+            nc.vector.tensor_copy(out=picked[:], in_=word_table[o][:].bitcast(U32).indirect(offs_sb[:]))
             return picked
 
-        w2_q = [quantise("w2_0", round_dealt("w2_0", w2_raw[0], False)[:], H)]
+        w2_q = [quantise_pass("w2_0", w2_raw[0])]
         x_picked = [gather_words(0)]
         x_scale = sb("x_scale", [P, S], U8)
-        nc.vector.tensor_copy(out=x_scale[:], in_=x_planes[:].indirect(offs_sb[:]))
-        w2_q.append(quantise("w2_1", round_dealt("w2_1", w2_raw[1], False)[:], H))
+        nc.vector.tensor_copy(out=x_scale[:], in_=scale_table[:].indirect(offs_sb[:]))
+        w2_q.append(quantise_pass("w2_1", w2_raw[1]))
         x_picked.append(gather_words(1))
 
-        def product(acc, w_q, o, t, cols):
+        def first_product(acc, w_q, o, t):
             codes, scales = w_q[o]
             nc.tensor.matmul_mx(
-                out=acc,
+                out=acc[:],
                 lhsT=codes[:, t * P : (t + 1) * P].bitcast(FP8X4),
                 lhsT_scale=scales[:, t * P : (t + 1) * P],
-                rhs=x_picked[o][:, cols].bitcast(FP8X4),
-                rhs_scale=x_scale[4 * o : P, cols],
+                rhs=x_picked[o][:].bitcast(FP8X4),
+                rhs_scale=x_scale[4 * o : P, :],
                 start=(o == 0),
                 stop=(o == PASSES - 1),
             )
@@ -128,15 +128,15 @@ def tile_picked_yhystr_sum_p_kernel(
         mg = [psum.tile([P, S], F32, name="mg%d" % t, tag="bank%d" % t) for t in range(PACK)]
         for o in range(PASSES):
             for t in range(PACK):
-                product(mg[t][:], w2_q, o, t, slice(0, S))
+                first_product(mg[t], w2_q, o, t)
 
         mag = []
         window = []
         for t in range(PACK):
-            table = sb("window%d" % t, [P, S + PAD], F32)
+            table = sb("window%d" % t, [P, S + SPARE], F32)
             nc.vector.memset(table[:, S:], 0.0)
             window.append(table)
-            if t in GATHER_ON_S:
+            if t >= FIRST_TILE_ON_SCALAR:
                 mag.append(table[:, :S])
                 nc.scalar.activation(out=mag[t], in_=mg[t][:], func=ACT.Tanh)
             else:
@@ -145,123 +145,100 @@ def tile_picked_yhystr_sum_p_kernel(
                 nc.scalar.activation(out=mag[t], in_=mg[t][:], func=ACT.Tanh)
                 nc.scalar.activation(out=table[:, :S], in_=mag[t], func=ACT.Copy, scale=0.5)
 
-
-        w1_q = [quantise("w1_0", round_dealt("w1_0", w1_raw[0], False)[:], H)]
-        w1_q.append(quantise("w1_1", round_dealt("w1_1", w1_raw[1], False)[:], H))
-
+        w1_q = [quantise_pass("w1_%d" % o, w1_raw[o]) for o in range(PASSES)]
         hf = [psum.tile([P, S], F32, name="hf%d" % t, tag="bank%d" % (PACK + t)) for t in range(PACK)]
         for t in range(PACK):
             for o in range(PASSES):
-                product(hf[t][:], w1_q, o, t, slice(0, S))
+                first_product(hf[t], w1_q, o, t)
 
         pin_gain = sb("pin_gain", [P, PACK], F32)
         slip_gain = sb("slip_gain", [P, PACK], F32)
         mag_gain = sb("mag_gain", [P, PACK], F32)
         w3_bf16 = sb("w3_bf16", [P, PACK * N], BF16)
+        hid = sb("hid", [P, PACK, S], F32)
+        near = {}
         w3_q = []
 
-        def late_constants():
-            nc.vector.scalar_tensor_tensor(
-                out=pin_gain[:], in0=kpin_sb[:], scalar=2.5, in1=unit_sb[:], op0=ALU.mult, op1=ALU.mult
-            )
-            nc.vector.tensor_scalar(out=slip_gain[:], in0=unit_sb[:], scalar1=0.4, scalar2=None, op0=ALU.mult)
-            nc.vector.tensor_scalar(out=mag_gain[:], in0=unit_sb[:], scalar1=1.4, scalar2=None, op0=ALU.mult)
+        def row_factors_and_w3_rounding():
+            nc.vector.tensor_tensor(pin_gain[:], kpin_sb[:, :, 0], unit_sb[:, :, 0], ALU.mult)
+            nc.vector.tensor_scalar(out=slip_gain[:], in0=unit_sb[:, :, 0], scalar1=0.4, scalar2=None, op0=ALU.mult)
+            nc.vector.tensor_scalar(out=mag_gain[:], in0=unit_sb[:, :, 0], scalar1=1.4, scalar2=None, op0=ALU.mult)
             nc.scalar.activation(
-                out=w3_bf16[:].rearrange("p (c i j) -> p c j i", i=4, j=PACK),
-                in_=w3_raw[:].rearrange("p j (c i) -> p c j i", i=4),
+                out=w3_bf16[:].rearrange("p (c e t) -> p c t e", e=RUN, t=PACK),
+                in_=w3_raw[:].rearrange("p t (c e) -> p c t e", e=RUN),
                 func=ACT.Copy,
             )
 
-        hid = sb("hid", [P, PACK, S], F32)
-        near = {}
-
         def neighbours(t):
-            one = sb("one%d" % t, [P, S], F32)
-            both = sb("both%d" % t, [P, S], F32)
-            if t in GATHER_ON_S:
-                two = sb("two%d" % t, [P, S], F32)
+            first = sb("first%d" % t, [P, S], F32)
+            near[t] = sb("near%d" % t, [P, S], F32)
+            if t >= FIRST_TILE_ON_SCALAR:
+                second = sb("second%d" % t, [P, S], F32)
                 pair = sb("pair%d" % t, [P, S], F32)
-                nc.scalar.activation(one[:], window[t][:].indirect(nn1_sb[:]), ACT.Copy)
-                nc.scalar.activation(two[:], window[t][:].indirect(nn2_sb[:]), ACT.Copy)
-                nc.vector.tensor_tensor(pair[:], one[:], two[:], ALU.add)
+                nc.scalar.activation(first[:], window[t][:].indirect(nn1_sb[:]), ACT.Copy)
+                nc.scalar.activation(second[:], window[t][:].indirect(nn2_sb[:]), ACT.Copy)
+                nc.vector.tensor_tensor(pair[:], first[:], second[:], ALU.add)
                 nc.vector.scalar_tensor_tensor(
-                    out=both[:], in0=pair[:], scalar=0.5, in1=mag[t], op0=ALU.mult, op1=ALU.add
+                    out=near[t][:], in0=pair[:], scalar=0.5, in1=mag[t], op0=ALU.mult, op1=ALU.add
                 )
             else:
-                nc.vector.tensor_tensor(one[:], window[t][:].indirect(nn1_sb[:]), mag[t], ALU.add)
-                nc.vector.tensor_tensor(both[:], window[t][:].indirect(nn2_sb[:]), one[:], ALU.add)
-            near[t] = both
+                nc.vector.tensor_tensor(first[:], window[t][:].indirect(nn1_sb[:]), mag[t], ALU.add)
+                nc.vector.tensor_tensor(near[t][:], window[t][:].indirect(nn2_sb[:]), first[:], ALU.add)
 
         def chain(n):
-            t, c0, c1 = UNITS[n]
+            t, c0, c1 = CHAINS[n]
 
-            def wt(name):
+            def step(name):
                 return sb("%s_%d" % (name, n), [P, c1 - c0], F32)
 
             if t not in near:
                 neighbours(t)
             mag_n = mag[t][:, c0:c1]
-            u = wt("u")
+            u = step("u")
             nc.vector.scalar_tensor_tensor(
                 out=u[:], in0=hf[t][:, c0:c1], scalar=1.0 / 0.6, in1=near[t][:, c0:c1], op0=ALU.mult, op1=ALU.add
             )
-
-            a, q, r = wt("a1"), wt("q1"), wt("r1")
-            if n in ABS_ON_V:
-                nc.vector.scalar_tensor_tensor(out=a[:], in0=u[:], scalar=-1.0, in1=u[:], op0=ALU.mult, op1=ALU.max)
+            abs_u, root_u, inv_u = step("abs_u"), step("root_u"), step("inv_u")
+            if n == 0:
+                nc.vector.scalar_tensor_tensor(
+                    out=abs_u[:], in0=u[:], scalar=-1.0, in1=u[:], op0=ALU.mult, op1=ALU.max
+                )
             else:
-                nc.scalar.activation(out=a[:], in_=u[:], func=ACT.Abs)
-            nc.scalar.activation(out=q[:], in_=a[:], func=ACT.Abs_reciprocal_sqrt, scale=0.75, bias=1.0)
-            nc.scalar.activation(out=r[:], in_=q[:], func=ACT.Square)
-            anh, d = wt("anh"), wt("d")
-            nc.vector.scalar_tensor_tensor(out=anh[:], in0=u[:], scalar=0.75, in1=r[:], op0=ALU.mult, op1=ALU.mult)
+                nc.scalar.activation(out=abs_u[:], in_=u[:], func=ACT.Abs)
+            nc.scalar.activation(out=root_u[:], in_=abs_u[:], func=ACT.Abs_reciprocal_sqrt, bias=0.8 / 0.6)
+            nc.scalar.activation(out=inv_u[:], in_=root_u[:], func=ACT.Square)
+            anh, d = step("anh"), step("d")
+            nc.vector.tensor_tensor(anh[:], u[:], inv_u[:], ALU.mult)
             nc.vector.tensor_tensor(d[:], anh[:], mag_n, ALU.subtract)
             if n == 0:
-                late_constants()
-            a2, q2, e, f = wt("a2"), wt("q2"), wt("e"), wt("f")
-            nc.scalar.activation(out=a2[:], in_=d[:], func=ACT.Abs)
-            if GAIN[n] == "X":
-                nc.scalar.activation(out=q2[:], in_=a2[:], func=ACT.Abs_reciprocal_sqrt, scale=2.5, bias=1.0)
-                nc.vector.scalar_tensor_tensor(
-                    out=e[:], in0=q2[:], scalar=pin_gain[:, t : t + 1], in1=q2[:], op0=ALU.mult, op1=ALU.mult
-                )
-                nc.vector.scalar_tensor_tensor(
-                    out=f[:], in0=e[:], scalar=slip_gain[:, t : t + 1], in1=d[:], op0=ALU.add, op1=ALU.mult
-                )
-            else:
-                r2 = wt("r2")
-                nc.scalar.activation(out=q2[:], in_=a2[:], func=ACT.Square, scale=2.5, bias=1.0)
-                nc.scalar.activation(out=r2[:], in_=q2[:], func=ACT.Abs_reciprocal_sqrt)
-                if GAIN[n] == "S":
-                    nc.scalar.activation(
-                        out=e[:], in_=r2[:], func=ACT.Identity,
-                        scale=pin_gain[:, t : t + 1], bias=slip_gain[:, t : t + 1],
-                    )
-                else:
-                    nc.vector.tensor_scalar(
-                        out=e[:], in0=r2[:], scalar1=pin_gain[:, t : t + 1],
-                        scalar2=slip_gain[:, t : t + 1], op0=ALU.mult, op1=ALU.add,
-                    )
-                nc.vector.tensor_tensor(f[:], d[:], e[:], ALU.mult)
+                row_factors_and_w3_rounding()
+            abs_d, root_d, pinned, moved = step("abs_d"), step("root_d"), step("pinned"), step("moved")
+            nc.scalar.activation(out=abs_d[:], in_=d[:], func=ACT.Abs)
+            nc.scalar.activation(out=root_d[:], in_=abs_d[:], func=ACT.Abs_reciprocal_sqrt, bias=0.4)
             nc.vector.scalar_tensor_tensor(
-                out=hid[:, t, c0:c1], in0=mag_n, scalar=mag_gain[:, t : t + 1], in1=f[:], op0=ALU.mult, op1=ALU.add
+                out=pinned[:], in0=root_d[:], scalar=pin_gain[:, t : t + 1], in1=root_d[:], op0=ALU.mult, op1=ALU.mult
+            )
+            nc.vector.scalar_tensor_tensor(
+                out=moved[:], in0=pinned[:], scalar=slip_gain[:, t : t + 1], in1=d[:], op0=ALU.add, op1=ALU.mult
+            )
+            nc.vector.scalar_tensor_tensor(
+                out=hid[:, t, c0:c1], in0=mag_n, scalar=mag_gain[:, t : t + 1], in1=moved[:], op0=ALU.mult, op1=ALU.add
             )
 
-
-        def coils(g):
-            c0, c1 = GROUPS[g]
-            width = c1 - c0
-            if g == 0:
-                w3_q.extend(quantise("w3", w3_bf16[:], N))
-            grouped = sb("hid_bf16_%d" % g, [P, PACK * width], BF16)
-            move(
-                IL[g] == "S",
-                grouped[:].rearrange("p (c i t) -> p c t i", i=4, t=PACK),
-                hid[:, :, c0:c1].rearrange("p t (c i) -> p c t i", i=4),
-            )
-            codes, scales = quantise("hid%d" % g, grouped[:], width)
-            acc = psum.tile([P, 2, width], F32, name="coil%d" % g, tag="bank%d" % g)
-            for m in range(2):
+        def coils(part):
+            cells = slice(part * OUT_COLS, (part + 1) * OUT_COLS)
+            if part == 0:
+                w3_q.extend(quantise("w3", w3_bf16, N))
+            rounded = sb("hid_bf16_%d" % part, [P, PACK * OUT_COLS], BF16)
+            dst = rounded[:].rearrange("p (c e t) -> p c t e", e=RUN, t=PACK)
+            src = hid[:, :, cells].rearrange("p t (c e) -> p c t e", e=RUN)
+            if part % 2 == 0:
+                nc.scalar.activation(out=dst, in_=src, func=ACT.Copy)
+            else:
+                nc.vector.tensor_copy(out=dst, in_=src)
+            codes, scales = quantise("hid%d" % part, rounded, OUT_COLS)
+            acc = psum.tile([P, N // P, OUT_COLS], F32, name="coil%d" % part, tag="bank%d" % part)
+            for m in range(N // P):
                 nc.tensor.matmul_mx(
                     out=acc[:, m, :],
                     lhsT=w3_q[0][:, m * P : (m + 1) * P].bitcast(FP8X4),
@@ -271,13 +248,12 @@ def tile_picked_yhystr_sum_p_kernel(
                     start=True,
                     stop=True,
                 )
-            result = sb("result%d" % g, [P, 2, width], F32)
-            move(EV[g] == "S", result[:], acc[:])
-            nc.sync.dma_start(out=out[:, c0:c1].rearrange("(m p) c -> p m c", p=P), in_=result[:])
+            result = sb("result%d" % part, [P, N // P, OUT_COLS], F32)
+            nc.scalar.activation(out=result[:], in_=acc[:], func=ACT.Copy)
+            nc.sync.dma_start(out=out[:, cells].rearrange("(m p) c -> p m c", p=P), in_=result[:])
 
-        for n, (t, c0, c1) in enumerate(UNITS):
+        for n, (t, c0, c1) in enumerate(CHAINS):
             chain(n)
             if t == PACK - 1:
-                for g, (g0, g1) in enumerate(GROUPS):
-                    if c0 < g1 <= c1:
-                        coils(g)
+                for part in range(c0 // OUT_COLS, c1 // OUT_COLS):
+                    coils(part)

@@ -185,7 +185,7 @@ def tile_picked_yhystr_sum_p_kernel(
                 nc.vector.tensor_tensor(first[:], window[t][:].indirect(nn1_sb[:]), mag[t], ALU.add)
                 nc.vector.tensor_tensor(near[t][:], window[t][:].indirect(nn2_sb[:]), first[:], ALU.add)
 
-        def chain(n):
+        def slip(n):
             t, c0, c1 = CHAINS[n]
 
             def step(name):
@@ -193,7 +193,6 @@ def tile_picked_yhystr_sum_p_kernel(
 
             if t not in near:
                 neighbours(t)
-            mag_n = mag[t][:, c0:c1]
             u = step("u")
             nc.vector.scalar_tensor_tensor(
                 out=u[:], in0=hf[t][:, c0:c1], scalar=1.0 / 0.6, in1=near[t][:, c0:c1], op0=ALU.mult, op1=ALU.add
@@ -209,20 +208,36 @@ def tile_picked_yhystr_sum_p_kernel(
             nc.scalar.activation(out=inv_u[:], in_=root_u[:], func=ACT.Square)
             anh, d = step("anh"), step("d")
             nc.vector.tensor_tensor(anh[:], u[:], inv_u[:], ALU.mult)
-            nc.vector.tensor_tensor(d[:], anh[:], mag_n, ALU.subtract)
+            nc.vector.tensor_tensor(d[:], anh[:], mag[t][:, c0:c1], ALU.subtract)
             if n == 0:
                 row_factors_and_w3_rounding()
-            abs_d, root_d, pinned, moved = step("abs_d"), step("root_d"), step("pinned"), step("moved")
+            abs_d, root_d = step("abs_d"), step("root_d")
             nc.scalar.activation(out=abs_d[:], in_=d[:], func=ACT.Abs)
             nc.scalar.activation(out=root_d[:], in_=abs_d[:], func=ACT.Abs_reciprocal_sqrt, bias=0.4)
+            return d, root_d
+
+        def hidden(n, d, root_d):
+            t, c0, c1 = CHAINS[n]
+            row = slice(t, t + 1)
+            gain = sb("gain_%d" % n, [P, c1 - c0], F32)
+            moved = sb("moved_%d" % n, [P, c1 - c0], F32)
+            if t == PACK - 1:
+                inv_d = sb("inv_d_%d" % n, [P, c1 - c0], F32)
+                nc.scalar.activation(out=inv_d[:], in_=root_d[:], func=ACT.Square)
+                nc.scalar.activation(
+                    out=gain[:], in_=inv_d[:], func=ACT.Identity, scale=pin_gain[:, row], bias=slip_gain[:, row]
+                )
+                nc.vector.tensor_tensor(moved[:], gain[:], d[:], ALU.mult)
+            else:
+                nc.vector.scalar_tensor_tensor(
+                    out=gain[:], in0=root_d[:], scalar=pin_gain[:, row], in1=root_d[:], op0=ALU.mult, op1=ALU.mult
+                )
+                nc.vector.scalar_tensor_tensor(
+                    out=moved[:], in0=gain[:], scalar=slip_gain[:, row], in1=d[:], op0=ALU.add, op1=ALU.mult
+                )
             nc.vector.scalar_tensor_tensor(
-                out=pinned[:], in0=root_d[:], scalar=pin_gain[:, t : t + 1], in1=root_d[:], op0=ALU.mult, op1=ALU.mult
-            )
-            nc.vector.scalar_tensor_tensor(
-                out=moved[:], in0=pinned[:], scalar=slip_gain[:, t : t + 1], in1=d[:], op0=ALU.add, op1=ALU.mult
-            )
-            nc.vector.scalar_tensor_tensor(
-                out=hid[:, t, c0:c1], in0=mag_n, scalar=mag_gain[:, t : t + 1], in1=moved[:], op0=ALU.mult, op1=ALU.add
+                out=hid[:, t, c0:c1], in0=mag[t][:, c0:c1], scalar=mag_gain[:, row], in1=moved[:],
+                op0=ALU.mult, op1=ALU.add,
             )
 
         def coils(part):
@@ -252,8 +267,9 @@ def tile_picked_yhystr_sum_p_kernel(
             nc.scalar.activation(out=result[:], in_=acc[:], func=ACT.Copy)
             nc.sync.dma_start(out=out[:, cells].rearrange("(m p) c -> p m c", p=P), in_=result[:])
 
+        slips = [slip(n) for n in range(len(CHAINS))]
         for n, (t, c0, c1) in enumerate(CHAINS):
-            chain(n)
+            hidden(n, *slips[n])
             if t == PACK - 1:
                 for part in range(c0 // OUT_COLS, c1 // OUT_COLS):
                     coils(part)

from contextlib import ExitStack

import concourse.mybir as mybir

K, T, S, N, H = 1024, 2048, 512, 256, 512
FLOPS = 2 * (2 * K * H * S + H * N * S)

F32 = mybir.dt.float32
BF16 = mybir.dt.bfloat16
I32 = mybir.dt.int32
U32 = mybir.dt.uint32
U16 = mybir.dt.uint16
U8 = mybir.dt.uint8
FP8X4 = mybir.dt.float8_e4m3fn_x4
ACT = mybir.ActivationFunctionType
ALU = mybir.AluOpType

P = 128
PACK = 4
RUN = 4
K_PASS = P * PACK
PASSES = K // K_PASS
QUADRANT = 32
SPARE = 16
FACTOR_PITCH = 8
OUT_COLS = 128

FIRST_TILE_ON_SCALAR = 2

CHAINS = [(t, 0, S) for t in range(PACK - 1)] + [(PACK - 1, 0, S // 2), (PACK - 1, S // 2, S)]

REUSE = {"abs_u_1": "abs_u_0", "pin_gain": "root_u_0", "slip_gain": "inv_u_0", "mag_gain": "anh_0"}


def tile_picked_yhystr_sum_p_kernel(
    tc, x_words, x_scales, w1, w2, kpin, unit, w3, offs, nn1, nn2, out
):
    nc = tc.nc
    with ExitStack() as ctx:
        keep = ctx.enter_context(tc.tile_pool(name="keep", bufs=1))
        psum = ctx.enter_context(tc.psum_pool(name="psum", bufs=1))

        def sb(name, shape, dtype):
            return keep.tile(shape, dtype, name=name, tag=REUSE.get(name, name), align_bytes=64)

        offs_sb = keep.tile([P, S // 16], U16, name="offs_sb")
        nn1_sb = keep.tile([P, S // 16], U16, name="nn1_sb")
        nn2_sb = keep.tile([P, S // 16], U16, name="nn2_sb")

        scale_table = sb("scale_table", [P, T], U8)
        nc.vector.memset(scale_table[:].bitcast(I32), 0)
        kpin_sb = sb("kpin_sb", [P, PACK, FACTOR_PITCH], F32)
        unit_sb = sb("unit_sb", [P, PACK, FACTOR_PITCH], F32)

        def load_pass(name, w, o):
            raw = sb("%s_raw%d" % (name, o), [P, PACK, H], F32)
            rows = w[o * K_PASS : (o + 1) * K_PASS, :]
            nc.sync.dma_start(out=raw[:], in_=rows.rearrange("(p j) c -> p j c", j=PACK))
            return raw

        def load_words(o):
            words = sb("word_table%d" % o, [P, T], I32)
            nc.sync.dma_start(out=words[:], in_=x_words[o].rearrange("p n j -> p (n j)").bitcast(I32))
            return words

        def by_tile(rows):
            return rows.rearrange("(g t e) n -> t g e n", t=PACK, e=RUN)

        w2_raw = [load_pass("w2", w2, 0)]
        for q in range(P // QUADRANT):
            nc.sync.dma_start(
                out=scale_table[QUADRANT * q : QUADRANT * q + 4 * PASSES, :].bitcast(I32),
                in_=x_scales[:, 4 * q : 4 * q + 4, :].bitcast(I32),
            )
        nc.sync.dma_start(offs_sb[:], offs)
        word_table = [load_words(0)]
        w2_raw.append(load_pass("w2", w2, 1))
        word_table.append(load_words(1))
        w1_raw = [load_pass("w1", w1, 0)]
        nc.sync.dma_start(nn1_sb[:], nn1)
        nc.sync.dma_start(nn2_sb[:], nn2)
        w1_raw.append(load_pass("w1", w1, 1))
        w3_raw = sb("w3_raw", [P, PACK, N], F32)
        for t in range(PACK):
            nc.sync.dma_start(out=w3_raw[:, t, :], in_=by_tile(w3)[t])
        for t in range(PACK):
            nc.sync.dma_start(out=kpin_sb[:, t, 0:1], in_=by_tile(kpin)[t])
            nc.sync.dma_start(out=unit_sb[:, t, 0:1], in_=by_tile(unit)[t])

        def quantise(name, rounded, width):
            codes = sb(name + "_codes", [P, width], U32)
            scales = sb(name + "_scales", [P, width], U8)
            nc.vector.quantize_mx(out=codes[:].bitcast(FP8X4), scales=scales[:], in_=rounded[:])
            return codes, scales

        def quantise_pass(name, raw):
            rounded = sb(name + "_bf16", [P, PACK * H], BF16)
            nc.vector.tensor_copy(
                out=rounded[:].rearrange("p (t g e j) -> p g t j e", t=PACK, e=RUN, j=PACK),
                in_=raw[:].rearrange("p j (g t e) -> p g t j e", t=PACK, e=RUN),
            )
            return quantise(name, rounded, H)

        def gather_words(o):
            picked = sb("x_picked%d" % o, [P, S], U32)
            nc.vector.tensor_copy(out=picked[:], in_=word_table[o][:].bitcast(U32).indirect(offs_sb[:]))
            return picked

        w2_q = [quantise_pass("w2_0", w2_raw[0])]
        x_picked = [gather_words(0)]
        x_scale = sb("x_scale", [P, S], U8)
        nc.vector.tensor_copy(out=x_scale[:], in_=scale_table[:].indirect(offs_sb[:]))
        w2_q.append(quantise_pass("w2_1", w2_raw[1]))
        x_picked.append(gather_words(1))

        def first_product(acc, w_q, o, t):
            codes, scales = w_q[o]
            nc.tensor.matmul_mx(
                out=acc[:],
                lhsT=codes[:, t * P : (t + 1) * P].bitcast(FP8X4),
                lhsT_scale=scales[:, t * P : (t + 1) * P],
                rhs=x_picked[o][:].bitcast(FP8X4),
                rhs_scale=x_scale[4 * o : P, :],
                start=(o == 0),
                stop=(o == PASSES - 1),
            )

        mg = [psum.tile([P, S], F32, name="mg%d" % t, tag="bank%d" % t) for t in range(PACK)]
        for o in range(PASSES):
            for t in range(PACK):
                first_product(mg[t], w2_q, o, t)

        mag = []
        window = []
        for t in range(PACK):
            table = sb("window%d" % t, [P, S + SPARE], F32)
            nc.vector.memset(table[:, S:], 0.0)
            window.append(table)
            if t >= FIRST_TILE_ON_SCALAR:
                mag.append(table[:, :S])
                nc.scalar.activation(out=mag[t], in_=mg[t][:], func=ACT.Tanh)
            else:
                plain = sb("mag%d" % t, [P, S], F32)
                mag.append(plain[:])
                nc.scalar.activation(out=mag[t], in_=mg[t][:], func=ACT.Tanh)
                nc.scalar.activation(out=table[:, :S], in_=mag[t], func=ACT.Copy, scale=0.5)

        w1_q = [quantise_pass("w1_%d" % o, w1_raw[o]) for o in range(PASSES)]
        hf = [psum.tile([P, S], F32, name="hf%d" % t, tag="bank%d" % (PACK + t)) for t in range(PACK)]
        for t in range(PACK):
            for o in range(PASSES):
                first_product(hf[t], w1_q, o, t)

        pin_gain = sb("pin_gain", [P, PACK], F32)
        slip_gain = sb("slip_gain", [P, PACK], F32)
        mag_gain = sb("mag_gain", [P, PACK], F32)
        w3_bf16 = sb("w3_bf16", [P, PACK * N], BF16)
        hid = sb("hid", [P, PACK, S], F32)
        near = {}
        w3_q = []

        def row_factors_and_w3_rounding():
            nc.vector.tensor_tensor(pin_gain[:], kpin_sb[:, :, 0], unit_sb[:, :, 0], ALU.mult)
            nc.vector.tensor_scalar(out=slip_gain[:], in0=unit_sb[:, :, 0], scalar1=0.4, scalar2=None, op0=ALU.mult)
            nc.vector.tensor_scalar(out=mag_gain[:], in0=unit_sb[:, :, 0], scalar1=1.4, scalar2=None, op0=ALU.mult)
            nc.scalar.activation(
                out=w3_bf16[:].rearrange("p (c e t) -> p c t e", e=RUN, t=PACK),
                in_=w3_raw[:].rearrange("p t (c e) -> p c t e", e=RUN),
                func=ACT.Copy,
            )

        def neighbours(t):
            first = sb("first%d" % t, [P, S], F32)
            near[t] = sb("near%d" % t, [P, S], F32)
            if t >= FIRST_TILE_ON_SCALAR:
                second = sb("second%d" % t, [P, S], F32)
                pair = sb("pair%d" % t, [P, S], F32)
                nc.scalar.activation(first[:], window[t][:].indirect(nn1_sb[:]), ACT.Copy)
                nc.scalar.activation(second[:], window[t][:].indirect(nn2_sb[:]), ACT.Copy)
                nc.vector.tensor_tensor(pair[:], first[:], second[:], ALU.add)
                nc.vector.scalar_tensor_tensor(
                    out=near[t][:], in0=pair[:], scalar=0.5, in1=mag[t], op0=ALU.mult, op1=ALU.add
                )
            else:
                nc.vector.tensor_tensor(first[:], window[t][:].indirect(nn1_sb[:]), mag[t], ALU.add)
                nc.vector.tensor_tensor(near[t][:], window[t][:].indirect(nn2_sb[:]), first[:], ALU.add)

        def slip(n):
            t, c0, c1 = CHAINS[n]

            def step(name):
                return sb("%s_%d" % (name, n), [P, c1 - c0], F32)

            if t not in near:
                neighbours(t)
            u = step("u")
            nc.vector.scalar_tensor_tensor(
                out=u[:], in0=hf[t][:, c0:c1], scalar=1.0 / 0.6, in1=near[t][:, c0:c1], op0=ALU.mult, op1=ALU.add
            )
            abs_u, root_u, inv_u = step("abs_u"), step("root_u"), step("inv_u")
            if n == 0:
                nc.vector.scalar_tensor_tensor(
                    out=abs_u[:], in0=u[:], scalar=-1.0, in1=u[:], op0=ALU.mult, op1=ALU.max
                )
            else:
                nc.scalar.activation(out=abs_u[:], in_=u[:], func=ACT.Abs)
            nc.scalar.activation(out=root_u[:], in_=abs_u[:], func=ACT.Abs_reciprocal_sqrt, bias=0.8 / 0.6)
            nc.scalar.activation(out=inv_u[:], in_=root_u[:], func=ACT.Square)
            anh, d = step("anh"), step("d")
            nc.vector.tensor_tensor(anh[:], u[:], inv_u[:], ALU.mult)
            nc.vector.tensor_tensor(d[:], anh[:], mag[t][:, c0:c1], ALU.subtract)
            if n == 0:
                row_factors_and_w3_rounding()
            abs_d, root_d = step("abs_d"), step("root_d")
            nc.scalar.activation(out=abs_d[:], in_=d[:], func=ACT.Abs)
            nc.scalar.activation(out=root_d[:], in_=abs_d[:], func=ACT.Abs_reciprocal_sqrt, bias=0.4)
            return d, root_d

        def hidden(n, d, root_d):
            t, c0, c1 = CHAINS[n]
            row = slice(t, t + 1)
            gain = sb("gain_%d" % n, [P, c1 - c0], F32)
            moved = sb("moved_%d" % n, [P, c1 - c0], F32)
            if t == PACK - 1:
                inv_d = sb("inv_d_%d" % n, [P, c1 - c0], F32)
                nc.scalar.activation(out=inv_d[:], in_=root_d[:], func=ACT.Square)
                nc.scalar.activation(
                    out=gain[:], in_=inv_d[:], func=ACT.Identity, scale=pin_gain[:, row], bias=slip_gain[:, row]
                )
                nc.vector.tensor_tensor(moved[:], gain[:], d[:], ALU.mult)
            else:
                nc.vector.scalar_tensor_tensor(
                    out=gain[:], in0=root_d[:], scalar=pin_gain[:, row], in1=root_d[:], op0=ALU.mult, op1=ALU.mult
                )
                nc.vector.scalar_tensor_tensor(
                    out=moved[:], in0=gain[:], scalar=slip_gain[:, row], in1=d[:], op0=ALU.add, op1=ALU.mult
                )
            nc.vector.scalar_tensor_tensor(
                out=hid[:, t, c0:c1], in0=mag[t][:, c0:c1], scalar=mag_gain[:, row], in1=moved[:],
                op0=ALU.mult, op1=ALU.add,
            )

        def coils(part):
            cells = slice(part * OUT_COLS, (part + 1) * OUT_COLS)
            if part == 0:
                w3_q.extend(quantise("w3", w3_bf16, N))
            rounded = sb("hid_bf16_%d" % part, [P, PACK * OUT_COLS], BF16)
            dst = rounded[:].rearrange("p (c e t) -> p c t e", e=RUN, t=PACK)
            src = hid[:, :, cells].rearrange("p t (c e) -> p c t e", e=RUN)
            if part % 2 == 0:
                nc.scalar.activation(out=dst, in_=src, func=ACT.Copy)
            else:
                nc.vector.tensor_copy(out=dst, in_=src)
            codes, scales = quantise("hid%d" % part, rounded, OUT_COLS)
            acc = psum.tile([P, N // P, OUT_COLS], F32, name="coil%d" % part, tag="bank%d" % part)
            for m in range(N // P):
                nc.tensor.matmul_mx(
                    out=acc[:, m, :],
                    lhsT=w3_q[0][:, m * P : (m + 1) * P].bitcast(FP8X4),
                    lhsT_scale=w3_q[1][:, m * P : (m + 1) * P],
                    rhs=codes[:].bitcast(FP8X4),
                    rhs_scale=scales[:],
                    start=True,
                    stop=True,
                )
            result = sb("result%d" % part, [P, N // P, OUT_COLS], F32)
            nc.scalar.activation(out=result[:], in_=acc[:], func=ACT.Copy)
            nc.sync.dma_start(out=out[:, cells].rearrange("(m p) c -> p m c", p=P), in_=result[:])

        slips = [slip(n) for n in range(len(CHAINS))]
        for n, (t, c0, c1) in enumerate(CHAINS):
            hidden(n, *slips[n])
            if t == PACK - 1:
                for part in range(c0 // OUT_COLS, c1 // OUT_COLS):
                    coils(part)
